import numpy as np
import ml_dtypes


def mxq(x, axis, fmt="e4m3"):
    dtype, down = {"e4m3": (ml_dtypes.float8_e4m3fn, 7), "e5m2": (ml_dtypes.float8_e5m2, 14)}[fmt]
    v = np.moveaxis(np.asarray(x, np.float32).astype(ml_dtypes.bfloat16).astype(np.float64), axis, -1)
    blocks = v.reshape(v.shape[:-1] + (-1, 32))
    amax = np.abs(blocks).max(-1, keepdims=True)
    byte = np.maximum(np.where(amax > 0, np.frexp(amax)[1] - 1 + 127, 0) - down, 1)
    scale = np.exp2(byte - 127.0)
    codes = (blocks / scale).astype(np.float32).astype(dtype).astype(np.float64)
    return np.moveaxis((codes * scale).reshape(v.shape), -1, axis)


WIDE = False


def mx_kscale(k):
    if not WIDE:
        return np.ones(k)
    levels = np.array([10, -10, 5, -5, 0])
    if k % 512:
        return np.exp2(np.random.permutation(np.resize(levels, k // 32))).repeat(32)
    a = np.empty((k // 512, 16))
    for p in range(k // 512):
        a[p, :8] = np.random.permutation(np.resize(levels, 8))
        for g in range(8):
            far = levels[np.abs(levels - a[p, g]) >= 10]
            a[p, g + 8] = far[np.random.randint(len(far))]
    return np.exp2(a.ravel()).repeat(32)


BF16 = ml_dtypes.bfloat16


def bf(x):
    return np.asarray(x, np.float32).astype(BF16)


def f64(x):
    return np.asarray(x).astype(np.float64)


E2M1 = np.array([0.0, 0.5, 1.0, 1.5, 2.0, 3.0, 4.0, 6.0, -0.0, -0.5, -1.0, -1.5, -2.0, -3.0, -4.0, -6.0])


def pack_weight(w, fmt):
    k, n = w.shape
    w = f64(bf(w)).reshape(k // 32, 32, n)
    amax = np.abs(w).max(1)
    if fmt == "e4m3":
        byte = np.frexp(amax)[1] - 1 + 127 - 7
    else:
        mant, ex = np.frexp(amax / 6.0)
        byte = np.where(mant > 0.5, ex, ex - 1) + 127
    byte = np.clip(np.where(amax > 0, byte, 1), 1, 254)
    scaled = (w * np.exp2(127.0 - byte)[:, None, :]).reshape(k, n).astype(np.float32)
    by_word = np.ascontiguousarray(scaled.reshape(k // 512, 128, 4, n).transpose(0, 1, 3, 2))
    if fmt == "e4m3":
        words = by_word.astype(ml_dtypes.float8_e4m3fn).view(np.uint8)
    else:
        c = by_word.astype(ml_dtypes.float4_e2m1fn).view(np.uint8) & 0xF
        words = c[..., 0::2] | (c[..., 1::2] << 4)
    return np.ascontiguousarray(words), np.ascontiguousarray(byte.astype(np.uint8).reshape(k // 512, 16, n))


def unpack_weight(words, scales, fmt):
    g, p, n, _ = words.shape
    if fmt == "e4m3":
        vals = np.ascontiguousarray(words).view(ml_dtypes.float8_e4m3fn).astype(np.float64)
    else:
        nib = np.empty((g, p, n, 4), np.uint8)
        nib[..., 0::2] = words & 0xF
        nib[..., 1::2] = words >> 4
        vals = E2M1[nib]
    vals = vals * np.repeat(np.exp2(scales.astype(np.float64) - 127.0), 8, axis=1)[..., None]
    return vals.transpose(0, 1, 3, 2).reshape(g * 512, n)
def pack4(w):
    words, scales = pack_weight(w, "e2m1")
    return words.reshape(words.shape[0], 128, -1), scales


def unpack4(words, scales):
    return unpack_weight(words.reshape(words.shape[0], 128, -1, 2), scales, "e2m1")


def planes(Y):
    n, m = Y.shape
    b = f64(bf(Y)).reshape(n // 32, 32, m)
    amax = np.abs(b).max(1)
    byte = np.clip(np.where(amax > 0, np.frexp(amax)[1] - 1 + 127 - 7, 1), 1, 254)
    codes = (b * np.exp2(127.0 - byte)[:, None, :]).reshape(n, m).astype(np.float32).astype(ml_dtypes.float8_e4m3fn).view(np.uint8)
    words = codes.reshape(n // 512, 128, 4, m).transpose(0, 1, 3, 2)
    return np.ascontiguousarray(words), np.ascontiguousarray(byte.astype(np.uint8).reshape(n // 512, 16, m))


PIX, BANDS, COMP = 768, 1024, 1536

def setup_inputs():
    s = mx_kscale(BANDS)
    spread = np.exp(0.7 * np.random.randn(COMP))
    XT = np.random.randn(BANDS, PIX)
    A = np.random.randn(BANDS, COMP) / np.sqrt(BANDS)
    C = np.random.randn(BANDS, COMP) / np.sqrt(BANDS) * spread
    E = np.random.randn(BANDS, COMP) / np.sqrt(BANDS) * spread
    x_words, x_scales = pack_weight(XT / s[:, None], "e4m3")
    a_words, a_scales = pack4(A * s[:, None])
    c_words, c_scales = pack_weight(C * s[:, None], "e4m3")
    return {
        "x_words": x_words, "x_scales": x_scales,
        "a_words": a_words, "a_scales": a_scales,
        "c_words": c_words, "c_scales": c_scales,
        "w_e": bf(E * s[:, None]),
        "pixel_scale": bf(np.exp(0.3 * np.random.randn(PIX))),
    }

def reference(x_words, x_scales, a_words, a_scales, c_words, c_scales, w_e, pixel_scale):
    XT = unpack_weight(x_words, x_scales, "e4m3")
    A = unpack4(a_words, a_scales)
    C = unpack_weight(c_words, c_scales, "e4m3")
    E = mxq(f64(w_e), 0, "e4m3")
    score = XT.T @ A
    coeff = XT.T @ C
    amp = XT.T @ E
    abundance = np.maximum(score, 0.0) * f64(pixel_scale)[:, None]
    y = coeff - abundance * amp
    Y = y.T
    words, scales = planes(Y)
    return y, words, scales

@@ -1,0 +1,320 @@
+from contextlib import ExitStack
+
+import concourse.mybir as mybir
+from concourse.masks import make_identity
+
+PIX, BANDS, COMP = 768, 1024, 1536
+FLOPS = 3 * 2 * PIX * BANDS * COMP
+
+F32 = mybir.dt.float32
+BF16 = mybir.dt.bfloat16
+I32 = mybir.dt.int32
+U32 = mybir.dt.uint32
+U8 = mybir.dt.uint8
+FP8X4 = mybir.dt.float8_e4m3fn_x4
+FP4X4 = mybir.dt.float4_e2m1fn_x4
+ALU = mybir.AluOpType
+ACT = mybir.ActivationFunctionType
+
+P = 128
+PASSES = BANDS // 512
+NC = 512
+GROUPS = COMP // NC
+PT = PIX // P
+TILES = GROUPS * PT
+LEAD = 7
+
+
+def tile_componentwise_unmixing_residual_k3_kernel(
+    tc, x_words, x_scales, a_words, a_scales, c_words, c_scales, w_e, pixel_scale, out_0, out_1, out_2
+):
+    nc = tc.nc
+    with ExitStack() as ctx:
+        keep = ctx.enter_context(tc.tile_pool(name="keep", bufs=1))
+        work = ctx.enter_context(tc.tile_pool(name="work", bufs=1))
+        psum = ctx.enter_context(tc.psum_pool(name="psum", bufs=2))
+        ctx.enter_context(tc.manual_schedule())
+
+        xs = keep.tile([P, PASSES, PIX], U8, align_bytes=64)
+        a_s = keep.tile([P, PASSES, COMP], U8, align_bytes=64)
+        c_s = keep.tile([P, COMP], U8, align_bytes=64)
+        x_w = keep.tile([P, PASSES, PIX], U32, align_bytes=64)
+        a_w = [keep.tile([P, PASSES, 2 * NC], U8, align_bytes=64, name="a_w%d" % j) for j in range(GROUPS)]
+        c_w = [keep.tile([P, PASSES, NC], U32, align_bytes=64, name="c_w%d" % j) for j in range(GROUPS)]
+        e_raw = {}
+        e_grp = {}
+        e_w = {}
+        e_s = {}
+        for j in range(GROUPS):
+            for g in range(PASSES):
+                e_raw[j, g] = keep.tile([P, 4, NC], BF16, align_bytes=64, name="e_raw%d%d" % (j, g))
+                e_grp[j, g] = keep.tile([P, NC, 4], BF16, align_bytes=64, name="e_grp%d%d" % (j, g))
+                e_w[j, g] = keep.tile([P, NC], U32, align_bytes=64, name="e_w%d%d" % (j, g))
+                e_s[j, g] = keep.tile([P, NC], U8, align_bytes=64, name="e_s%d%d" % (j, g))
+        y_w = [keep.tile([P, PIX], U32, align_bytes=64, name="y_w%d" % j) for j in range(GROUPS)]
+        y_s01 = keep.tile([P, PIX], U8, align_bytes=64)
+        y_s2 = keep.tile([P, PIX], U8, align_bytes=64)
+        ident = keep.tile([P, P], F32)
+        ps_rows = keep.tile([P, P], BF16)
+        ps_rows32 = keep.tile([P, P], F32)
+        ps = keep.tile([P, PT], F32)
+        table = keep.tile([P, 1], F32)
+
+        xw = x_words.rearrange("g p n t -> p g (n t)").bitcast(I32)
+        aw = a_words.rearrange("g p n -> p g n").bitcast(I32)
+        cw = c_words.rearrange("g p n t -> p g (n t)").bitcast(I32)
+
+        def load_a(j):
+            nc.sync.dma_start(out=a_w[j][:].bitcast(I32), in_=aw[:, :, j * NC // 2 : (j + 1) * NC // 2])
+
+        def load_c(j):
+            nc.sync.dma_start(out=c_w[j][:].bitcast(I32), in_=cw[:, :, j * NC : (j + 1) * NC])
+
+        def load_e(j, g):
+            rows = w_e[512 * g : 512 * (g + 1), j * NC : (j + 1) * NC]
+            nc.sync.dma_start(out=e_raw[j, g][:], in_=rows.rearrange("(p t) n -> p t n", t=4))
+
+        def interleave_e(copy, j, g, n0, n1):
+            copy(
+                out=e_grp[j, g][:, n0:n1, :].rearrange("p (c i) t -> p c t i", i=4),
+                in_=e_raw[j, g][:, :, n0:n1].rearrange("p t (c i) -> p c t i", i=4),
+            )
+
+        def quantize_e(j, g, n0, n1):
+            nc.vector.quantize_mx(
+                out=e_w[j, g][:, n0:n1].bitcast(FP8X4),
+                scales=e_s[j, g][:, n0:n1],
+                in_=e_grp[j, g][:, n0:n1, :].rearrange("p n t -> p (n t)"),
+            )
+
+        def product(acc, k, rhs, rhs_scale):
+            m0 = (k % PT) * P
+            for g in range(PASSES):
+                nc.tensor.matmul_mx(
+                    out=acc,
+                    lhsT=x_w[:, g, m0 : m0 + P].bitcast(FP8X4),
+                    lhsT_scale=xs[:, g, m0 : m0 + P],
+                    rhs=rhs(g),
+                    rhs_scale=rhs_scale(g),
+                    start=(g == 0),
+                    stop=(g == PASSES - 1),
+                )
+
+        half = NC // 2
+        quarter = NC // 4
+        relu = {}
+        prod = {}
+        y16 = {}
+        y_grp = {}
+
+        def score(k, tag):
+            j = k // PT
+            acc = psum.tile([P, NC], F32, name="score_acc", tag=tag)
+            product(acc[:], k, lambda g: a_w[j][:, g, :].bitcast(FP4X4), lambda g: a_s[:, g, j * NC : (j + 1) * NC])
+            relu[k] = work.tile([P, NC], F32, name="relu", tag="relu", bufs=LEAD + 3)
+            nc.scalar.activation(out=relu[k][:], in_=acc[:], func=ACT.Relu)
+
+        def amp(k):
+            j = k // PT
+            acc = psum.tile([P, NC], F32, name="amp_acc", tag="amp")
+            product(acc[:], k, lambda g: e_w[j, g][:].bitcast(FP8X4), lambda g: e_s[j, g][:])
+            prod[k] = work.tile([P, NC], F32, name="prod", tag="prod", bufs=3)
+            i = k % PT
+            nc.vector.scalar_tensor_tensor(
+                out=prod[k][:], in0=relu[k][:], scalar=ps[:, i : i + 1], in1=acc[:], op0=ALU.mult, op1=ALU.mult
+            )
+
+        def coeff(k):
+            j = k // PT
+            acc = psum.tile([P, NC], F32, name="coeff_acc", tag="coeff")
+            product(
+                acc[:], k, lambda g: c_w[j][:, g, :].bitcast(FP8X4), lambda g: c_s[4 + 4 * g :, j * NC : (j + 1) * NC]
+            )
+            y32 = work.tile([P, NC], F32, name="y32", tag="y32", bufs=8)
+            nc.vector.tensor_tensor(out=y32[:], in0=acc[:], in1=prod[k][:], op=ALU.subtract)
+            return y32
+
+        def round_and_store(k, y32):
+            j, i = divmod(k, PT)
+            y16[k] = work.tile([P, 2, P, 2], BF16, name="y16", tag="y16", bufs=8)
+            nc.scalar.copy(out=y16[k][:], in_=y32[:].rearrange("m (p u e) -> m u p e", u=2, e=2))
+            nc.sync.dma_start(out=out_0[i * P : (i + 1) * P, j * NC : (j + 1) * NC], in_=y32[:])
+
+        def last_tile():
+            k = TILES - 1
+            j, i = divmod(k, PT)
+            y16[k] = work.tile([P, 2, P, 2], BF16, name="y16", tag="y16", bufs=8)
+            y32 = work.tile([P, NC], F32, name="y32", tag="y32", bufs=8)
+            halves = []
+            for h, tag in enumerate(("coeff", "score")):
+                n0 = h * half
+                acc = psum.tile([P, half], F32, name="half_acc", tag=tag)
+                product(
+                    acc[:],
+                    k,
+                    lambda g: c_w[j][:, g, n0 : n0 + half].bitcast(FP8X4),
+                    lambda g: c_s[4 + 4 * g :, j * NC + n0 : j * NC + n0 + half],
+                )
+                nc.vector.tensor_tensor(
+                    out=y16[k][:, :, h * P // 2 : (h + 1) * P // 2, :],
+                    in0=acc[:].rearrange("m (p u e) -> m u p e", u=2, e=2),
+                    in1=prod[k][:, n0 : n0 + half].rearrange("m (p u e) -> m u p e", u=2, e=2),
+                    op=ALU.subtract,
+                )
+                halves.append((n0, acc))
+            for n0, acc in halves:
+                nc.vector.tensor_tensor(
+                    out=y32[:, n0 : n0 + half], in0=acc[:], in1=prod[k][:, n0 : n0 + half], op=ALU.subtract
+                )
+            nc.sync.dma_start(out=out_0[i * P : (i + 1) * P, j * NC : (j + 1) * NC], in_=y32[:])
+
+        def turn(k0, n, tag):
+            bank = psum.tile([P, 2, 2, P], F32, name="turned", tag=tag)
+            for a in range(n):
+                words = y16[k0 + a][:].rearrange("m u p e -> m u (p e)").bitcast(F32)
+                for u in range(2):
+                    nc.tensor.transpose(bank[:, a, u, :], words[:, u, :], ident[:])
+            return bank
+
+        def gather(k0, n, bank):
+            y_grp[k0] = work.tile([P, 2 * P, 4], BF16, name="y_grp", tag="y_grp", bufs=4, align_bytes=64)
+            nc.scalar.copy(
+                out=y_grp[k0][:, : n * P, :].bitcast(F32).rearrange("p (a m) u -> p a m u", a=n),
+                in_=bank[:, :n].rearrange("p a u m -> p a m u"),
+            )
+
+        def quantize_y(k0, n):
+            j, i = divmod(k0, PT)
+            cols = slice(i * P, (i + n) * P)
+            plane = y_s01[4 * j :, cols] if j < 2 else y_s2[:, cols]
+            nc.vector.quantize_mx(
+                out=y_w[j][:, cols].bitcast(FP8X4),
+                scales=plane,
+                in_=y_grp[k0][:, : n * P, :].rearrange("p m t -> p (m t)"),
+            )
+
+        def store_words(queue, j, m0, m1):
+            dst = out_1[j].rearrange("p m t -> p (m t)").bitcast(I32)
+            queue.dma_start(out=dst[:, m0:m1], in_=y_w[j][:, m0:m1].bitcast(I32))
+
+        def load_x_scales(queue, q):
+            queue.dma_start(
+                out=xs[32 * q : 32 * q + 4].bitcast(I32),
+                in_=x_scales[:, 4 * q : 4 * q + 4, :].rearrange("g r n -> r g n").bitcast(I32),
+            )
+
+        def load_a_scales(queue, q):
+            queue.dma_start(
+                out=a_s[32 * q : 32 * q + 4].bitcast(I32),
+                in_=a_scales[:, 4 * q : 4 * q + 4, :].rearrange("g r n -> r g n").bitcast(I32),
+            )
+
+        nc.gpsimd.memset(ps_rows[:], 0.0)
+        nc.gpsimd.dma_start(out=ps_rows[:PT, :], in_=pixel_scale.rearrange("(i p) -> i p", p=P))
+        nc.vector.memset(xs[:].bitcast(I32), 0)
+        nc.vector.memset(a_s[:].bitcast(I32), 0)
+        nc.vector.memset(ident[:], 0.0)
+        nc.vector.memset(table[:], 0.0)
+        nc.vector.memset(c_s[:].bitcast(I32), 0)
+        load_a(0)
+        for q in range(4):
+            load_x_scales(nc.scalar, q)
+        for q in range(2):
+            load_a_scales(nc.scalar, q)
+        nc.sync.dma_start(out=x_w[:].bitcast(I32), in_=xw)
+        load_a_scales(nc.scalar, 2)
+        load_a_scales(nc.gpsimd, 3)
+        make_identity(nc, ident[:], nomemset=True)
+        nc.scalar.activation(out=table[:], in_=table[:], func=ACT.Relu)
+        load_e(0, 0)
+        load_e(0, 1)
+        load_a(1)
+        for q in range(4):
+            nc.sync.dma_start(
+                out=c_s[32 * q + 4 : 32 * q + 12, :].bitcast(I32),
+                in_=c_scales[:, 4 * q : 4 * q + 4, :].bitcast(I32),
+            )
+        load_c(0)
+        load_e(1, 0)
+        load_e(1, 1)
+        load_a(2)
+        load_c(1)
+        load_e(2, 0)
+        load_e(2, 1)
+        load_c(2)
+
+        nc.vector.tensor_copy(out=ps_rows32[:], in_=ps_rows[:])
+        ps_bank = psum.tile([P, P], F32, name="ps_bank", tag="amp")
+        nc.tensor.transpose(ps_bank[:], ps_rows32[:], ident[:])
+        nc.vector.tensor_copy(out=ps[:], in_=ps_bank[:, :PT])
+
+        vcopy = nc.vector.tensor_copy
+        scopy = nc.scalar.copy
+        for g in range(PASSES):
+            interleave_e(vcopy, 0, g, 0, half)
+            interleave_e(vcopy, 0, g, half, NC)
+            quantize_e(0, g, 0, half)
+            quantize_e(0, g, half, NC)
+        for k in range(LEAD):
+            score(k, "score" if k % 2 == 0 else "turn")
+
+        s_pieces = []
+        for j in range(1, GROUPS):
+            s_pieces.extend([(j, 0, h) for h in range(4)] + [(j, 1, h) for h in range(2)])
+
+        def scalar_piece():
+            j, g, h = s_pieces[0]
+            s_pieces.remove((j, g, h))
+            interleave_e(scopy, j, g, h * quarter, (h + 1) * quarter)
+
+        for h in range(4):
+            scalar_piece()
+        turns = {5: [(0, 2), (2, 2)], 9: [(4, 2), (6, 2)], 13: [(8, 2), (10, 2)], 15: [(12, 2)]}
+        scored = LEAD
+        amp(0)
+        for k in range(TILES - 1):
+            amp(k + 1)
+            y32 = coeff(k)
+            if k % 3 != 2 and scored < TILES:
+                score(scored, "score")
+                scored = scored + 1
+            round_and_store(k, y32)
+            for k0, n in turns.get(k - 2, []):
+                quantize_y(k0, n)
+                if k0 == 4 or k0 == 10:
+                    store_words(nc.sync, k0 // PT, 0, PIX)
+                if k0 == 10:
+                    for q in range(4):
+                        nc.sync.dma_start(
+                            out=out_2[0:2, 4 * q : 4 * q + 4, :].bitcast(I32),
+                            in_=y_s01[32 * q : 32 * q + 8, :].bitcast(I32),
+                        )
+            j, r = divmod(k, PT)
+            if j + 1 < GROUPS:
+                if r == 0:
+                    interleave_e(vcopy, j + 1, 1, half, NC)
+                if r == 1:
+                    quantize_e(j + 1, 0, 0, NC)
+                if r == 3:
+                    quantize_e(j + 1, 1, 0, NC)
+            banks = [(k0, n, turn(k0, n, "turn")) for k0, n in turns.get(k, [])]
+            for k0, n, bank in banks:
+                gather(k0, n, bank)
+            if s_pieces:
+                scalar_piece()
+        last_tile()
+        quantize_y(12, 2)
+        tail = [(14, 2, "turn"), (16, 1, "turn"), (17, 1, "amp")]
+        banks = [(k0, n, turn(k0, n, tag)) for k0, n, tag in tail]
+        for k0, n, bank in banks:
+            gather(k0, n, bank)
+            quantize_y(k0, n)
+            if k0 == 14:
+                store_words(nc.sync, 2, 0, 4 * P)
+        store_words(nc.sync, 2, 4 * P, PIX)
+        for q in range(4):
+            queue = nc.scalar if q % 2 == 0 else nc.sync
+            queue.dma_start(
+                out=out_2[2, 4 * q : 4 * q + 4, :].bitcast(I32),
+                in_=y_s2[32 * q : 32 * q + 4, :].bitcast(I32),
+            )

@@ -22,7 +22,8 @@ NC = 512
 GROUPS = COMP // NC
 PT = PIX // P
 TILES = GROUPS * PT
-LEAD = 7
+X_HEAD = 256
+LEAD = 9
 
 
 def tile_componentwise_unmixing_residual_k3_kernel(
@@ -36,9 +37,11 @@ def tile_componentwise_unmixing_residual_k3_kernel(
         ctx.enter_context(tc.manual_schedule())
 
         xs = keep.tile([P, PASSES, PIX], U8, align_bytes=64)
-        a_s = keep.tile([P, PASSES, COMP], U8, align_bytes=64)
+        a_s0 = keep.tile([P, PASSES, NC], U8, align_bytes=64)
+        a_s12 = keep.tile([P, PASSES, COMP - NC], U8, align_bytes=64)
         c_s = keep.tile([P, COMP], U8, align_bytes=64)
-        x_w = keep.tile([P, PASSES, PIX], U32, align_bytes=64)
+        x_head = keep.tile([P, PASSES, X_HEAD], U32, align_bytes=64)
+        x_rest = keep.tile([P, PASSES, PIX - X_HEAD], U32, align_bytes=64)
         a_w = [keep.tile([P, PASSES, 2 * NC], U8, align_bytes=64, name="a_w%d" % j) for j in range(GROUPS)]
         c_w = [keep.tile([P, PASSES, NC], U32, align_bytes=64, name="c_w%d" % j) for j in range(GROUPS)]
         e_raw = {}
@@ -90,9 +93,13 @@ def tile_componentwise_unmixing_residual_k3_kernel(
         def product(acc, k, rhs, rhs_scale):
             m0 = (k % PT) * P
             for g in range(PASSES):
+                if m0 < X_HEAD:
+                    lhs = x_head[:, g, m0 : m0 + P]
+                else:
+                    lhs = x_rest[:, g, m0 - X_HEAD : m0 - X_HEAD + P]
                 nc.tensor.matmul_mx(
                     out=acc,
-                    lhsT=x_w[:, g, m0 : m0 + P].bitcast(FP8X4),
+                    lhsT=lhs.bitcast(FP8X4),
                     lhsT_scale=xs[:, g, m0 : m0 + P],
                     rhs=rhs(g),
                     rhs_scale=rhs_scale(g),
@@ -110,7 +117,7 @@ def tile_componentwise_unmixing_residual_k3_kernel(
         def score(k, tag):
             j = k // PT
             acc = psum.tile([P, NC], F32, name="score_acc", tag=tag)
-            product(acc[:], k, lambda g: a_w[j][:, g, :].bitcast(FP4X4), lambda g: a_s[:, g, j * NC : (j + 1) * NC])
+            product(acc[:], k, lambda g: a_w[j][:, g, :].bitcast(FP4X4), lambda g: a_s0[:, g, :] if j == 0 else a_s12[:, g, (j - 1) * NC : j * NC])
             relu[k] = work.tile([P, NC], F32, name="relu", tag="relu", bufs=LEAD + 3)
             nc.scalar.activation(out=relu[k][:], in_=acc[:], func=ACT.Relu)
 
@@ -203,38 +210,40 @@ def tile_componentwise_unmixing_residual_k3_kernel(
                 in_=x_scales[:, 4 * q : 4 * q + 4, :].rearrange("g r n -> r g n").bitcast(I32),
             )
 
-        def load_a_scales(queue, q):
+        def load_a_scales(queue, plane, cols, q):
             queue.dma_start(
-                out=a_s[32 * q : 32 * q + 4].bitcast(I32),
-                in_=a_scales[:, 4 * q : 4 * q + 4, :].rearrange("g r n -> r g n").bitcast(I32),
+                out=plane[32 * q : 32 * q + 4].bitcast(I32),
+                in_=a_scales[:, 4 * q : 4 * q + 4, cols].rearrange("g r n -> r g n").bitcast(I32),
             )
 
-        nc.gpsimd.memset(ps_rows[:], 0.0)
-        nc.gpsimd.dma_start(out=ps_rows[:PT, :], in_=pixel_scale.rearrange("(i p) -> i p", p=P))
         nc.vector.memset(xs[:].bitcast(I32), 0)
-        nc.vector.memset(a_s[:].bitcast(I32), 0)
-        nc.vector.memset(ident[:], 0.0)
+        nc.vector.memset(a_s0[:].bitcast(I32), 0)
+        nc.gpsimd.memset(ps_rows[:], 0.0)
         nc.vector.memset(table[:], 0.0)
+        nc.vector.memset(a_s12[:].bitcast(I32), 0)
         nc.vector.memset(c_s[:].bitcast(I32), 0)
-        load_a(0)
-        for q in range(4):
-            load_x_scales(nc.scalar, q)
-        for q in range(2):
-            load_a_scales(nc.scalar, q)
-        nc.sync.dma_start(out=x_w[:].bitcast(I32), in_=xw)
-        load_a_scales(nc.scalar, 2)
-        load_a_scales(nc.gpsimd, 3)
-        make_identity(nc, ident[:], nomemset=True)
         nc.scalar.activation(out=table[:], in_=table[:], func=ACT.Relu)
+        nc.gpsimd.dma_start(out=ps_rows[:PT, :], in_=pixel_scale.rearrange("(i p) -> i p", p=P))
+        make_identity(nc, ident[:])
+        load_a(0)
+        for q in range(3):
+            load_x_scales(nc.sync, q)
+        nc.sync.dma_start(out=x_head[:].bitcast(I32), in_=xw[:, :, :X_HEAD])
+        load_x_scales(nc.sync, 3)
+        for q in range(4):
+            load_a_scales(nc.sync, a_s0, slice(0, NC), q)
         load_e(0, 0)
+        nc.sync.dma_start(out=x_rest[:].bitcast(I32), in_=xw[:, :, X_HEAD:])
         load_e(0, 1)
         load_a(1)
+        for q in range(4):
+            load_a_scales(nc.sync, a_s12, slice(NC, COMP), q)
+        load_c(0)
         for q in range(4):
             nc.sync.dma_start(
                 out=c_s[32 * q + 4 : 32 * q + 12, :].bitcast(I32),
                 in_=c_scales[:, 4 * q : 4 * q + 4, :].bitcast(I32),
             )
-        load_c(0)
         load_e(1, 0)
         load_e(1, 1)
         load_a(2)
@@ -244,9 +253,9 @@ def tile_componentwise_unmixing_residual_k3_kernel(
         load_c(2)
 
         nc.vector.tensor_copy(out=ps_rows32[:], in_=ps_rows[:])
-        ps_bank = psum.tile([P, P], F32, name="ps_bank", tag="amp")
+        ps_bank = psum.tile([P, P], F32, name="ps_bank", tag="coeff")
         nc.tensor.transpose(ps_bank[:], ps_rows32[:], ident[:])
-        nc.vector.tensor_copy(out=ps[:], in_=ps_bank[:, :PT])
+        nc.scalar.copy(out=ps[:], in_=ps_bank[:, :PT])
 
         vcopy = nc.vector.tensor_copy
         scopy = nc.scalar.copy
@@ -270,14 +279,14 @@ def tile_componentwise_unmixing_residual_k3_kernel(
         for h in range(4):
             scalar_piece()
         turns = {5: [(0, 2), (2, 2)], 9: [(4, 2), (6, 2)], 13: [(8, 2), (10, 2)], 15: [(12, 2)]}
-        scored = LEAD
+        late = TILES - LEAD
+        score_step = {1 + n * (TILES - 2) // late: LEAD + n for n in range(late)}
         amp(0)
         for k in range(TILES - 1):
             amp(k + 1)
             y32 = coeff(k)
-            if k % 3 != 2 and scored < TILES:
-                score(scored, "score")
-                scored = scored + 1
+            if k in score_step:
+                score(score_step[k], "score")
             round_and_store(k, y32)
             for k0, n in turns.get(k - 2, []):
                 quantize_y(k0, n)

@@ -22,8 +22,8 @@ NC = 512
 GROUPS = COMP // NC
 PT = PIX // P
 TILES = GROUPS * PT
-X_HEAD = 256
-LEAD = 9
+X_HEAD = 384
+LEAD = 10
 
 
 def tile_componentwise_unmixing_residual_k3_kernel(
@@ -206,14 +206,14 @@ def tile_componentwise_unmixing_residual_k3_kernel(
 
         def load_x_scales(queue, q):
             queue.dma_start(
-                out=xs[32 * q : 32 * q + 4].bitcast(I32),
-                in_=x_scales[:, 4 * q : 4 * q + 4, :].rearrange("g r n -> r g n").bitcast(I32),
+                out=xs[q:P:32].bitcast(I32),
+                in_=x_scales[:, q:16:4, :].rearrange("g r n -> r g n").bitcast(I32),
             )
 
         def load_a_scales(queue, plane, cols, q):
             queue.dma_start(
-                out=plane[32 * q : 32 * q + 4].bitcast(I32),
-                in_=a_scales[:, 4 * q : 4 * q + 4, cols].rearrange("g r n -> r g n").bitcast(I32),
+                out=plane[q:P:32].bitcast(I32),
+                in_=a_scales[:, q:16:4, cols].rearrange("g r n -> r g n").bitcast(I32),
             )
 
         nc.vector.memset(xs[:].bitcast(I32), 0)
@@ -225,6 +225,8 @@ def tile_componentwise_unmixing_residual_k3_kernel(
         nc.scalar.activation(out=table[:], in_=table[:], func=ACT.Relu)
         nc.gpsimd.dma_start(out=ps_rows[:PT, :], in_=pixel_scale.rearrange("(i p) -> i p", p=P))
         make_identity(nc, ident[:])
+        for q in range(4):
+            load_a_scales(nc.gpsimd, a_s12, slice(NC, COMP), q)
         load_a(0)
         for q in range(3):
             load_x_scales(nc.sync, q)
@@ -236,8 +238,6 @@ def tile_componentwise_unmixing_residual_k3_kernel(
         nc.sync.dma_start(out=x_rest[:].bitcast(I32), in_=xw[:, :, X_HEAD:])
         load_e(0, 1)
         load_a(1)
-        for q in range(4):
-            load_a_scales(nc.sync, a_s12, slice(NC, COMP), q)
         load_c(0)
         for q in range(4):
             nc.sync.dma_start(
@@ -278,9 +278,8 @@ def tile_componentwise_unmixing_residual_k3_kernel(
 
         for h in range(4):
             scalar_piece()
-        turns = {5: [(0, 2), (2, 2)], 9: [(4, 2), (6, 2)], 13: [(8, 2), (10, 2)], 15: [(12, 2)]}
-        late = TILES - LEAD
-        score_step = {1 + n * (TILES - 2) // late: LEAD + n for n in range(late)}
+        turns = {6: [(0, 2), (2, 2)], 10: [(4, 2), (6, 2)], 13: [(8, 2), (10, 2)], 15: [(12, 2)]}
+        score_step = {2 * n: LEAD + n for n in range(TILES - LEAD)}
         amp(0)
         for k in range(TILES - 1):
             amp(k + 1)

@@ -37,8 +37,7 @@ def tile_componentwise_unmixing_residual_k3_kernel(
         ctx.enter_context(tc.manual_schedule())
 
         xs = keep.tile([P, PASSES, PIX], U8, align_bytes=64)
-        a_s0 = keep.tile([P, PASSES, NC], U8, align_bytes=64)
-        a_s12 = keep.tile([P, PASSES, COMP - NC], U8, align_bytes=64)
+        a_s = keep.tile([P, PASSES, COMP], U8, align_bytes=64)
         c_s = keep.tile([P, COMP], U8, align_bytes=64)
         x_head = keep.tile([P, PASSES, X_HEAD], U32, align_bytes=64)
         x_rest = keep.tile([P, PASSES, PIX - X_HEAD], U32, align_bytes=64)
@@ -117,7 +116,7 @@ def tile_componentwise_unmixing_residual_k3_kernel(
         def score(k, tag):
             j = k // PT
             acc = psum.tile([P, NC], F32, name="score_acc", tag=tag)
-            product(acc[:], k, lambda g: a_w[j][:, g, :].bitcast(FP4X4), lambda g: a_s0[:, g, :] if j == 0 else a_s12[:, g, (j - 1) * NC : j * NC])
+            product(acc[:], k, lambda g: a_w[j][:, g, :].bitcast(FP4X4), lambda g: a_s[:, g, j * NC : (j + 1) * NC])
             relu[k] = work.tile([P, NC], F32, name="relu", tag="relu", bufs=LEAD + 3)
             nc.scalar.activation(out=relu[k][:], in_=acc[:], func=ACT.Relu)
 
@@ -210,34 +209,31 @@ def tile_componentwise_unmixing_residual_k3_kernel(
                 in_=x_scales[:, q:16:4, :].rearrange("g r n -> r g n").bitcast(I32),
             )
 
-        def load_a_scales(queue, plane, cols, q):
+        def load_a_scales(queue, q):
             queue.dma_start(
-                out=plane[q:P:32].bitcast(I32),
-                in_=a_scales[:, q:16:4, cols].rearrange("g r n -> r g n").bitcast(I32),
+                out=a_s[q:P:32].bitcast(I32),
+                in_=a_scales[:, q:16:4, :].rearrange("g r n -> r g n").bitcast(I32),
             )
 
         nc.vector.memset(xs[:].bitcast(I32), 0)
-        nc.vector.memset(a_s0[:].bitcast(I32), 0)
+        nc.vector.memset(a_s[:].bitcast(I32), 0)
         nc.gpsimd.memset(ps_rows[:], 0.0)
         nc.vector.memset(table[:], 0.0)
-        nc.vector.memset(a_s12[:].bitcast(I32), 0)
         nc.vector.memset(c_s[:].bitcast(I32), 0)
         nc.scalar.activation(out=table[:], in_=table[:], func=ACT.Relu)
         nc.gpsimd.dma_start(out=ps_rows[:PT, :], in_=pixel_scale.rearrange("(i p) -> i p", p=P))
         make_identity(nc, ident[:])
-        for q in range(4):
-            load_a_scales(nc.gpsimd, a_s12, slice(NC, COMP), q)
         load_a(0)
         for q in range(3):
             load_x_scales(nc.sync, q)
         nc.sync.dma_start(out=x_head[:].bitcast(I32), in_=xw[:, :, :X_HEAD])
         load_x_scales(nc.sync, 3)
         for q in range(4):
-            load_a_scales(nc.sync, a_s0, slice(0, NC), q)
+            load_a_scales(nc.sync, q)
         load_e(0, 0)
         nc.sync.dma_start(out=x_rest[:].bitcast(I32), in_=xw[:, :, X_HEAD:])
-        load_e(0, 1)
         load_a(1)
+        load_e(0, 1)
         load_c(0)
         for q in range(4):
             nc.sync.dma_start(

from contextlib import ExitStack

import concourse.mybir as mybir
from concourse.masks import make_identity

PIX, BANDS, COMP = 768, 1024, 1536
FLOPS = 3 * 2 * PIX * BANDS * COMP

F32 = mybir.dt.float32
BF16 = mybir.dt.bfloat16
I32 = mybir.dt.int32
U32 = mybir.dt.uint32
U8 = mybir.dt.uint8
FP8X4 = mybir.dt.float8_e4m3fn_x4
FP4X4 = mybir.dt.float4_e2m1fn_x4
ALU = mybir.AluOpType
ACT = mybir.ActivationFunctionType

P = 128
PASSES = BANDS // 512
NC = 512
GROUPS = COMP // NC
PT = PIX // P
TILES = GROUPS * PT
X_HEAD = 384
LEAD = 10


def tile_componentwise_unmixing_residual_k3_kernel(
    tc, x_words, x_scales, a_words, a_scales, c_words, c_scales, w_e, pixel_scale, out_0, out_1, out_2
):
    nc = tc.nc
    with ExitStack() as ctx:
        keep = ctx.enter_context(tc.tile_pool(name="keep", bufs=1))
        work = ctx.enter_context(tc.tile_pool(name="work", bufs=1))
        psum = ctx.enter_context(tc.psum_pool(name="psum", bufs=2))
        ctx.enter_context(tc.manual_schedule())

        xs = keep.tile([P, PASSES, PIX], U8, align_bytes=64)
        a_s = keep.tile([P, PASSES, COMP], U8, align_bytes=64)
        c_s = keep.tile([P, COMP], U8, align_bytes=64)
        x_head = keep.tile([P, PASSES, X_HEAD], U32, align_bytes=64)
        x_rest = keep.tile([P, PASSES, PIX - X_HEAD], U32, align_bytes=64)
        a_w = [keep.tile([P, PASSES, 2 * NC], U8, align_bytes=64, name="a_w%d" % j) for j in range(GROUPS)]
        c_w = [keep.tile([P, PASSES, NC], U32, align_bytes=64, name="c_w%d" % j) for j in range(GROUPS)]
        e_raw = {}
        e_grp = {}
        e_w = {}
        e_s = {}
        for j in range(GROUPS):
            for g in range(PASSES):
                e_raw[j, g] = keep.tile([P, 4, NC], BF16, align_bytes=64, name="e_raw%d%d" % (j, g))
                e_grp[j, g] = keep.tile([P, NC, 4], BF16, align_bytes=64, name="e_grp%d%d" % (j, g))
                e_w[j, g] = keep.tile([P, NC], U32, align_bytes=64, name="e_w%d%d" % (j, g))
                e_s[j, g] = keep.tile([P, NC], U8, align_bytes=64, name="e_s%d%d" % (j, g))
        y_w = [keep.tile([P, PIX], U32, align_bytes=64, name="y_w%d" % j) for j in range(GROUPS)]
        y_s01 = keep.tile([P, PIX], U8, align_bytes=64)
        y_s2 = keep.tile([P, PIX], U8, align_bytes=64)
        ident = keep.tile([P, P], F32)
        ps_rows = keep.tile([P, P], BF16)
        ps_rows32 = keep.tile([P, P], F32)
        ps = keep.tile([P, PT], F32)
        table = keep.tile([P, 1], F32)

        xw = x_words.rearrange("g p n t -> p g (n t)").bitcast(I32)
        aw = a_words.rearrange("g p n -> p g n").bitcast(I32)
        cw = c_words.rearrange("g p n t -> p g (n t)").bitcast(I32)

        def load_a(j):
            nc.sync.dma_start(out=a_w[j][:].bitcast(I32), in_=aw[:, :, j * NC // 2 : (j + 1) * NC // 2])

        def load_c(j):
            nc.sync.dma_start(out=c_w[j][:].bitcast(I32), in_=cw[:, :, j * NC : (j + 1) * NC])

        def load_e(j, g):
            rows = w_e[512 * g : 512 * (g + 1), j * NC : (j + 1) * NC]
            nc.sync.dma_start(out=e_raw[j, g][:], in_=rows.rearrange("(p t) n -> p t n", t=4))

        def interleave_e(copy, j, g, n0, n1):
            copy(
                out=e_grp[j, g][:, n0:n1, :].rearrange("p (c i) t -> p c t i", i=4),
                in_=e_raw[j, g][:, :, n0:n1].rearrange("p t (c i) -> p c t i", i=4),
            )

        def quantize_e(j, g, n0, n1):
            nc.vector.quantize_mx(
                out=e_w[j, g][:, n0:n1].bitcast(FP8X4),
                scales=e_s[j, g][:, n0:n1],
                in_=e_grp[j, g][:, n0:n1, :].rearrange("p n t -> p (n t)"),
            )

        def product(acc, k, rhs, rhs_scale):
            m0 = (k % PT) * P
            for g in range(PASSES):
                if m0 < X_HEAD:
                    lhs = x_head[:, g, m0 : m0 + P]
                else:
                    lhs = x_rest[:, g, m0 - X_HEAD : m0 - X_HEAD + P]
                nc.tensor.matmul_mx(
                    out=acc,
                    lhsT=lhs.bitcast(FP8X4),
                    lhsT_scale=xs[:, g, m0 : m0 + P],
                    rhs=rhs(g),
                    rhs_scale=rhs_scale(g),
                    start=(g == 0),
                    stop=(g == PASSES - 1),
                )

        half = NC // 2
        quarter = NC // 4
        relu = {}
        prod = {}
        y16 = {}
        y_grp = {}

        def score(k, tag):
            j = k // PT
            acc = psum.tile([P, NC], F32, name="score_acc", tag=tag)
            product(acc[:], k, lambda g: a_w[j][:, g, :].bitcast(FP4X4), lambda g: a_s[:, g, j * NC : (j + 1) * NC])
            relu[k] = work.tile([P, NC], F32, name="relu", tag="relu", bufs=LEAD + 3)
            nc.scalar.activation(out=relu[k][:], in_=acc[:], func=ACT.Relu)

        def amp(k):
            j = k // PT
            acc = psum.tile([P, NC], F32, name="amp_acc", tag="amp")
            product(acc[:], k, lambda g: e_w[j, g][:].bitcast(FP8X4), lambda g: e_s[j, g][:])
            prod[k] = work.tile([P, NC], F32, name="prod", tag="prod", bufs=3)
            i = k % PT
            nc.vector.scalar_tensor_tensor(
                out=prod[k][:], in0=relu[k][:], scalar=ps[:, i : i + 1], in1=acc[:], op0=ALU.mult, op1=ALU.mult
            )

        def coeff(k):
            j = k // PT
            acc = psum.tile([P, NC], F32, name="coeff_acc", tag="coeff")
            product(
                acc[:], k, lambda g: c_w[j][:, g, :].bitcast(FP8X4), lambda g: c_s[4 + 4 * g :, j * NC : (j + 1) * NC]
            )
            y32 = work.tile([P, NC], F32, name="y32", tag="y32", bufs=8)
            nc.vector.tensor_tensor(out=y32[:], in0=acc[:], in1=prod[k][:], op=ALU.subtract)
            return y32

        def round_and_store(k, y32):
            j, i = divmod(k, PT)
            y16[k] = work.tile([P, 2, P, 2], BF16, name="y16", tag="y16", bufs=8)
            nc.scalar.copy(out=y16[k][:], in_=y32[:].rearrange("m (p u e) -> m u p e", u=2, e=2))
            nc.sync.dma_start(out=out_0[i * P : (i + 1) * P, j * NC : (j + 1) * NC], in_=y32[:])

        def last_tile():
            k = TILES - 1
            j, i = divmod(k, PT)
            y16[k] = work.tile([P, 2, P, 2], BF16, name="y16", tag="y16", bufs=8)
            y32 = work.tile([P, NC], F32, name="y32", tag="y32", bufs=8)
            halves = []
            for h, tag in enumerate(("coeff", "score")):
                n0 = h * half
                acc = psum.tile([P, half], F32, name="half_acc", tag=tag)
                product(
                    acc[:],
                    k,
                    lambda g: c_w[j][:, g, n0 : n0 + half].bitcast(FP8X4),
                    lambda g: c_s[4 + 4 * g :, j * NC + n0 : j * NC + n0 + half],
                )
                nc.vector.tensor_tensor(
                    out=y16[k][:, :, h * P // 2 : (h + 1) * P // 2, :],
                    in0=acc[:].rearrange("m (p u e) -> m u p e", u=2, e=2),
                    in1=prod[k][:, n0 : n0 + half].rearrange("m (p u e) -> m u p e", u=2, e=2),
                    op=ALU.subtract,
                )
                halves.append((n0, acc))
            for n0, acc in halves:
                nc.vector.tensor_tensor(
                    out=y32[:, n0 : n0 + half], in0=acc[:], in1=prod[k][:, n0 : n0 + half], op=ALU.subtract
                )
            nc.sync.dma_start(out=out_0[i * P : (i + 1) * P, j * NC : (j + 1) * NC], in_=y32[:])

        def turn(k0, n, tag):
            bank = psum.tile([P, 2, 2, P], F32, name="turned", tag=tag)
            for a in range(n):
                words = y16[k0 + a][:].rearrange("m u p e -> m u (p e)").bitcast(F32)
                for u in range(2):
                    nc.tensor.transpose(bank[:, a, u, :], words[:, u, :], ident[:])
            return bank

        def gather(k0, n, bank):
            y_grp[k0] = work.tile([P, 2 * P, 4], BF16, name="y_grp", tag="y_grp", bufs=4, align_bytes=64)
            nc.scalar.copy(
                out=y_grp[k0][:, : n * P, :].bitcast(F32).rearrange("p (a m) u -> p a m u", a=n),
                in_=bank[:, :n].rearrange("p a u m -> p a m u"),
            )

        def quantize_y(k0, n):
            j, i = divmod(k0, PT)
            cols = slice(i * P, (i + n) * P)
            plane = y_s01[4 * j :, cols] if j < 2 else y_s2[:, cols]
            nc.vector.quantize_mx(
                out=y_w[j][:, cols].bitcast(FP8X4),
                scales=plane,
                in_=y_grp[k0][:, : n * P, :].rearrange("p m t -> p (m t)"),
            )

        def store_words(queue, j, m0, m1):
            dst = out_1[j].rearrange("p m t -> p (m t)").bitcast(I32)
            queue.dma_start(out=dst[:, m0:m1], in_=y_w[j][:, m0:m1].bitcast(I32))

        def load_x_scales(queue, q):
            queue.dma_start(
                out=xs[q:P:32].bitcast(I32),
                in_=x_scales[:, q:16:4, :].rearrange("g r n -> r g n").bitcast(I32),
            )

        def load_a_scales(queue, q):
            queue.dma_start(
                out=a_s[q:P:32].bitcast(I32),
                in_=a_scales[:, q:16:4, :].rearrange("g r n -> r g n").bitcast(I32),
            )

        nc.vector.memset(xs[:].bitcast(I32), 0)
        nc.vector.memset(a_s[:].bitcast(I32), 0)
        nc.gpsimd.memset(ps_rows[:], 0.0)
        nc.vector.memset(table[:], 0.0)
        nc.vector.memset(c_s[:].bitcast(I32), 0)
        nc.scalar.activation(out=table[:], in_=table[:], func=ACT.Relu)
        nc.gpsimd.dma_start(out=ps_rows[:PT, :], in_=pixel_scale.rearrange("(i p) -> i p", p=P))
        make_identity(nc, ident[:])
        load_a(0)
        for q in range(3):
            load_x_scales(nc.sync, q)
        nc.sync.dma_start(out=x_head[:].bitcast(I32), in_=xw[:, :, :X_HEAD])
        load_x_scales(nc.sync, 3)
        for q in range(4):
            load_a_scales(nc.sync, q)
        load_e(0, 0)
        nc.sync.dma_start(out=x_rest[:].bitcast(I32), in_=xw[:, :, X_HEAD:])
        load_a(1)
        load_e(0, 1)
        load_c(0)
        for q in range(4):
            nc.sync.dma_start(
                out=c_s[32 * q + 4 : 32 * q + 12, :].bitcast(I32),
                in_=c_scales[:, 4 * q : 4 * q + 4, :].bitcast(I32),
            )
        load_e(1, 0)
        load_e(1, 1)
        load_a(2)
        load_c(1)
        load_e(2, 0)
        load_e(2, 1)
        load_c(2)

        nc.vector.tensor_copy(out=ps_rows32[:], in_=ps_rows[:])
        ps_bank = psum.tile([P, P], F32, name="ps_bank", tag="coeff")
        nc.tensor.transpose(ps_bank[:], ps_rows32[:], ident[:])
        nc.scalar.copy(out=ps[:], in_=ps_bank[:, :PT])

        vcopy = nc.vector.tensor_copy
        scopy = nc.scalar.copy
        for g in range(PASSES):
            interleave_e(vcopy, 0, g, 0, half)
            interleave_e(vcopy, 0, g, half, NC)
            quantize_e(0, g, 0, half)
            quantize_e(0, g, half, NC)
        for k in range(LEAD):
            score(k, "score" if k % 2 == 0 else "turn")

        s_pieces = []
        for j in range(1, GROUPS):
            s_pieces.extend([(j, 0, h) for h in range(4)] + [(j, 1, h) for h in range(2)])

        def scalar_piece():
            j, g, h = s_pieces[0]
            s_pieces.remove((j, g, h))
            interleave_e(scopy, j, g, h * quarter, (h + 1) * quarter)

        for h in range(4):
            scalar_piece()
        turns = {6: [(0, 2), (2, 2)], 10: [(4, 2), (6, 2)], 13: [(8, 2), (10, 2)], 15: [(12, 2)]}
        score_step = {2 * n: LEAD + n for n in range(TILES - LEAD)}
        amp(0)
        for k in range(TILES - 1):
            amp(k + 1)
            y32 = coeff(k)
            if k in score_step:
                score(score_step[k], "score")
            round_and_store(k, y32)
            for k0, n in turns.get(k - 2, []):
                quantize_y(k0, n)
                if k0 == 4 or k0 == 10:
                    store_words(nc.sync, k0 // PT, 0, PIX)
                if k0 == 10:
                    for q in range(4):
                        nc.sync.dma_start(
                            out=out_2[0:2, 4 * q : 4 * q + 4, :].bitcast(I32),
                            in_=y_s01[32 * q : 32 * q + 8, :].bitcast(I32),
                        )
            j, r = divmod(k, PT)
            if j + 1 < GROUPS:
                if r == 0:
                    interleave_e(vcopy, j + 1, 1, half, NC)
                if r == 1:
                    quantize_e(j + 1, 0, 0, NC)
                if r == 3:
                    quantize_e(j + 1, 1, 0, NC)
            banks = [(k0, n, turn(k0, n, "turn")) for k0, n in turns.get(k, [])]
            for k0, n, bank in banks:
                gather(k0, n, bank)
            if s_pieces:
                scalar_piece()
        last_tile()
        quantize_y(12, 2)
        tail = [(14, 2, "turn"), (16, 1, "turn"), (17, 1, "amp")]
        banks = [(k0, n, turn(k0, n, tag)) for k0, n, tag in tail]
        for k0, n, bank in banks:
            gather(k0, n, bank)
            quantize_y(k0, n)
            if k0 == 14:
                store_words(nc.sync, 2, 0, 4 * P)
        store_words(nc.sync, 2, 4 * P, PIX)
        for q in range(4):
            queue = nc.scalar if q % 2 == 0 else nc.sync
            queue.dma_start(
                out=out_2[2, 4 * q : 4 * q + 4, :].bitcast(I32),
                in_=y_s2[32 * q : 32 * q + 4, :].bitcast(I32),
            )
